import numpy as np
import ml_dtypes


def mxq(x, axis, fmt="e4m3"):
    dtype, down = {"e4m3": (ml_dtypes.float8_e4m3fn, 7), "e5m2": (ml_dtypes.float8_e5m2, 14)}[fmt]
    v = np.moveaxis(np.asarray(x, np.float32).astype(ml_dtypes.bfloat16).astype(np.float64), axis, -1)
    blocks = v.reshape(v.shape[:-1] + (-1, 32))
    amax = np.abs(blocks).max(-1, keepdims=True)
    byte = np.maximum(np.where(amax > 0, np.frexp(amax)[1] - 1 + 127, 0) - down, 1)
    scale = np.exp2(byte - 127.0)
    codes = (blocks / scale).astype(np.float32).astype(dtype).astype(np.float64)
    return np.moveaxis((codes * scale).reshape(v.shape), -1, axis)


WIDE = False


def mx_kscale(k):
    if not WIDE:
        return np.ones(k)
    levels = np.array([10, -10, 5, -5, 0])
    if k % 512:
        return np.exp2(np.random.permutation(np.resize(levels, k // 32))).repeat(32)
    a = np.empty((k // 512, 16))
    for p in range(k // 512):
        a[p, :8] = np.random.permutation(np.resize(levels, 8))
        for g in range(8):
            far = levels[np.abs(levels - a[p, g]) >= 10]
            a[p, g + 8] = far[np.random.randint(len(far))]
    return np.exp2(a.ravel()).repeat(32)


def f64(x):
    return np.asarray(x).astype(np.float64)


def striped(idx):
    return np.tile(idx.reshape(-1, 16).T, (8, 1)).astype(np.uint16)


def unstriped(offs):
    return offs[:16].T.reshape(-1).astype(np.int64)


def pack_weight(w):
    k, n = w.shape
    w = f64(np.asarray(w, np.float32).astype(ml_dtypes.bfloat16)).reshape(k // 32, 32, n)
    amax = np.abs(w).max(1)
    byte = np.clip(np.where(amax > 0, np.frexp(amax)[1] - 1 + 127 - 7, 1), 1, 254)
    scaled = (w * np.exp2(127.0 - byte)[:, None, :]).reshape(k, n).astype(np.float32)
    words = np.ascontiguousarray(scaled.reshape(k // 512, 128, 4, n).transpose(0, 1, 3, 2)).astype(ml_dtypes.float8_e4m3fn).view(np.uint8)
    return words, np.ascontiguousarray(byte.astype(np.uint8).reshape(k // 512, 16, n))


def unpack_weight(words, scales):
    g, p, n, _ = words.shape
    vals = np.ascontiguousarray(words).view(ml_dtypes.float8_e4m3fn).astype(np.float64) * np.repeat(np.exp2(scales.astype(np.float64) - 127.0), 8, axis=1)[..., None]
    return vals.transpose(0, 1, 3, 2).reshape(g * 512, n)


def gelu(v):
    return 0.5 * v * (1.0 + np.tanh(np.sqrt(2.0 / np.pi) * (v + 0.044715 * v**3)))


K, T, S, V, H, N = 1024, 2048, 512, 256, 512, 256


def setup_inputs():
    n = np.random.standard_normal
    s = mx_kscale(K)[:, None]
    u = mx_kscale(H)
    packed_w2 = pack_weight(n((H, N)) / np.sqrt(2 * H) / u[:, None])
    packed_w3 = pack_weight(n((H, N)) / np.sqrt(2 * H) / u[:, None])
    return {
        "xT": (n((K, T)) * s).astype(np.float32),
        "w1": (n((K, H)) / np.sqrt(K) / s * u).astype(np.float32),
        "w2_words": packed_w2[0],
        "w2_scales": packed_w2[1],
        "w3_words": packed_w3[0],
        "w3_scales": packed_w3[1],
        "offs": striped(np.random.permutation(T)[:S]),
    }


def reference(xT, w1, w2_words, w2_scales, w3_words, w3_scales, offs):
    xq = mxq(f64(xT)[:, unstriped(offs)], 0, "e4m3")
    h = gelu(mxq(f64(w1), 0, "e4m3").T @ xq)
    low = 0.5 * (h[:, :V] + h[:, V:2 * V])
    high = 0.5 * (h[:, :V] - h[:, V:2 * V])
    return unpack_weight(w2_words, w2_scales).T @ mxq(low, 0, "e4m3") + unpack_weight(w3_words, w3_scales).T @ mxq(high, 0, "e4m3")

@@ -1,0 +1,175 @@
+from contextlib import ExitStack
+
+import concourse.mybir as mybir
+
+K, T, S, V, H, N = 1024, 2048, 512, 256, 512, 256
+FLOPS = 2 * K * H * S + 2 * 2 * H * N * V
+
+F32 = mybir.dt.float32
+BF16 = mybir.dt.bfloat16
+I32 = mybir.dt.int32
+U32 = mybir.dt.uint32
+U16 = mybir.dt.uint16
+U8 = mybir.dt.uint8
+FP8X4 = mybir.dt.float8_e4m3fn_x4
+GELU = mybir.ActivationFunctionType.Gelu_apprx_tanh
+ADD = mybir.AluOpType.add
+SUB = mybir.AluOpType.subtract
+
+P = 128
+PACK = 4
+K_PASS = P * PACK
+GROUPS = 4
+PAIRS = V // GROUPS
+
+
+def tile_picked_haar_gelu_e_kernel(tc, xT, w1, w2_words, w2_scales, w3_words, w3_scales, offs, out):
+    nc = tc.nc
+    with ExitStack() as ctx:
+        sb = ctx.enter_context(tc.tile_pool(name="sb", bufs=1))
+        ps = ctx.enter_context(tc.psum_pool(name="ps", bufs=1))
+
+        def sbuf(name, shape, dtype):
+            return sb.tile(shape, dtype, name=name, align_bytes=64)
+
+        def quantize(codes, scales, values):
+            nc.vector.quantize_mx(out=codes.bitcast(FP8X4), scales=scales, in_=values)
+
+        offsets = sb.tile([P, S // 16], U16, name="offsets")
+
+        warm_in = sbuf("warm_in", [P, 1], F32)
+        warm_out = sbuf("warm_out", [P, 1], F32)
+        nc.vector.memset(warm_in[:], 0.0)
+        nc.scalar.activation(warm_out[:], warm_in[:], GELU)
+
+        band_scales = []
+        for name, scales in (("w2", w2_scales), ("w3", w3_scales)):
+            plane = sbuf(name + "_plane", [P, N], U8)
+            nc.gpsimd.memset(plane[:], 0)
+            for q in range(4):
+                nc.gpsimd.dma_start(out=plane[32 * q : 32 * q + 4, :].bitcast(I32), in_=scales[0, 4 * q : 4 * q + 4, :].bitcast(I32))
+            band_scales.append(plane)
+
+        x_rows = xT.rearrange("(z p j) t -> z j p t", z=2, j=PACK)
+        w_rows = w1.rearrange("(z p j) c -> z p j c", z=2, j=PACK)
+        planes = {}
+
+        def load_plane(z, j):
+            planes[z, j] = sbuf("x_%d_%d" % (z, j), [P, T], F32)
+            nc.sync.dma_start(out=planes[z, j][:], in_=x_rows[z, j])
+
+        load_plane(0, 0)
+        nc.sync.dma_start(offsets[:], offs)
+        w_first = sbuf("w_first", [P, PACK, H], F32)
+        nc.sync.dma_start(out=w_first[:], in_=w_rows[0])
+        for z in range(2):
+            for j in range(PACK):
+                if (z, j) != (0, 0):
+                    load_plane(z, j)
+        w_last = []
+        for half in range(2):
+            raw = sbuf("w_last_%d" % half, [P, PACK, H // 2], F32)
+            nc.sync.dma_start(out=raw[:], in_=w_rows[1][:, :, half * (H // 2) : (half + 1) * (H // 2)])
+            w_last.append(raw)
+        band_words = []
+        for name, words in (("w2", w2_words), ("w3", w3_words)):
+            tile = sbuf(name + "_codes", [P, N], I32)
+            nc.sync.dma_start(out=tile[:], in_=words[0].rearrange("p n r -> p (n r)").bitcast(I32))
+            band_words.append(tile)
+
+        w_codes = [sbuf("w_codes_%d" % z, [P, H], U32) for z in range(2)]
+        w_scales = [sbuf("w_scales_%d" % z, [P, H], U8) for z in range(2)]
+        x_codes = {}
+        x_scales = {}
+        picked = [sbuf("picked_%d" % z, [P, S, PACK], BF16) for z in range(2)]
+
+        def gather(z):
+            for j in range(PACK):
+                nc.vector.tensor_copy(
+                    out=picked[z][:, :, j].rearrange("p (g d v) -> p d g v", g=GROUPS, d=2),
+                    in_=planes[z, j][:].indirect(offsets[:]),
+                )
+
+        def quantize_picked(z, half):
+            x_codes[z, half] = sbuf("x_codes_%d_%d" % (z, half), [P, S // 2], U32)
+            x_scales[z, half] = sbuf("x_scales_%d_%d" % (z, half), [P, S // 2], U8)
+            values = picked[z][:, half * (S // 2) : (half + 1) * (S // 2), :].rearrange("p s j -> p (s j)")
+            quantize(x_codes[z, half][:], x_scales[z, half][:], values)
+
+        hidden = [ps.tile([P, PACK, P], F32, name="hidden_%d" % g) for g in range(GROUPS)]
+
+        def first_product(z, g):
+            cols = slice((g % 2) * P, (g % 2 + 1) * P)
+            for t in range(PACK):
+                nc.tensor.matmul_mx(
+                    out=hidden[g][:, t, :],
+                    lhsT=w_codes[z][:, t * P : (t + 1) * P].bitcast(FP8X4),
+                    lhsT_scale=w_scales[z][:, t * P : (t + 1) * P],
+                    rhs=x_codes[z, g // 2][:, cols].bitcast(FP8X4),
+                    rhs_scale=x_scales[z, g // 2][:, cols],
+                    start=(z == 0 and t == 0),
+                    stop=(z == 1 and t == PACK - 1),
+                )
+
+        w_bf = sbuf("w_bf", [P, PACK, P, PACK], BF16)
+        nc.scalar.copy(out=w_bf[:].rearrange("p t m j -> p m j t"), in_=w_first[:].rearrange("p j (m t) -> p m j t", t=PACK))
+        quantize(w_codes[0][:], w_scales[0][:], w_bf[:].rearrange("p t m j -> p (t m j)"))
+        gather(0)
+        for half in range(2):
+            quantize_picked(0, half)
+        for g in range(GROUPS):
+            first_product(0, g)
+
+        gather(1)
+        quantize_picked(1, 0)
+        for half in range(2):
+            for pair in range(2):
+                piece = sbuf("w_bf_%d_%d" % (half, pair), [P, 2, P // 2, PACK], BF16)
+                source = w_last[half][:].rearrange("p j (m t) -> p m j t", t=PACK)[:, :, :, 2 * pair : 2 * pair + 2]
+                target = piece[:].rearrange("p t m j -> p m j t")
+                if half == 1 and pair == 0:
+                    nc.vector.tensor_copy(out=target, in_=source)
+                else:
+                    nc.scalar.copy(out=target, in_=source)
+                for u in range(2):
+                    first = (2 * pair + u) * P + half * (P // 2)
+                    cols = slice(first, first + P // 2)
+                    quantize(w_codes[1][:, cols], w_scales[1][:, cols], piece[:, u].rearrange("p m j -> p (m j)"))
+        quantize_picked(1, 1)
+
+        out_rows = out.rearrange("(a p) v -> p a v", p=P)
+        for half in range(2):
+            codes = [sbuf("band_codes_%d_%d" % (half, b), [P, P], U32) for b in range(2)]
+            scales = [sbuf("band_scales_%d_%d" % (half, b), [P, P], U8) for b in range(2)]
+            for g in range(2 * half, 2 * half + 2):
+                first_product(1, g)
+                h = sbuf("h_%d" % g, [P, 2, PAIRS * PACK], F32)
+                nc.scalar.activation(
+                    h[:].rearrange("p d (v t) -> p (d v) t", t=PACK), hidden[g][:].rearrange("p t n -> p n t"), GELU
+                )
+                bands = [sbuf("band_%d_%d" % (g, b), [P, PAIRS * PACK], BF16) for b in range(2)]
+                for b, op in enumerate((ADD, SUB)):
+                    nc.vector.tensor_tensor(bands[b][:], h[:, 0, :], h[:, 1, :], op)
+                cols = slice((g % 2) * PAIRS, (g % 2 + 1) * PAIRS)
+                for b in range(2):
+                    quantize(codes[b][:, cols], scales[b][:, cols], bands[b][:])
+            for a in range(2):
+                acc = ps.tile([P, P], F32, name="acc_%d_%d" % (half, a))
+                for b in range(2):
+                    nc.tensor.matmul_mx(
+                        out=acc[:],
+                        lhsT=band_words[b][:, a * P : (a + 1) * P].bitcast(FP8X4),
+                        lhsT_scale=band_scales[b][:, a * P : (a + 1) * P],
+                        rhs=codes[b][:].bitcast(FP8X4),
+                        rhs_scale=scales[b][:],
+                        start=(b == 0),
+                        stop=(b == 1),
+                    )
+                result = sbuf("result_%d_%d" % (half, a), [P, P], F32)
+                if half == 1 and a == 1:
+                    nc.vector.tensor_scalar_mul(result[:], acc[:], 0.5)
+                    nc.sync.dma_start(out=out_rows[:, a, half * P : (half + 1) * P], in_=result[:])
+                else:
+                    nc.scalar.mul(result[:], acc[:], 0.5)
+                    queue = nc.scalar if half == 1 else nc.sync
+                    queue.dma_start(out=out_rows[:, a, half * P : (half + 1) * P], in_=result[:])

@@ -21,6 +21,7 @@ PACK = 4
 K_PASS = P * PACK
 GROUPS = 4
 PAIRS = V // GROUPS
+VECTOR_SHARE = 40
 
 
 def tile_picked_haar_gelu_e_kernel(tc, xT, w1, w2_words, w2_scales, w3_words, w3_scales, offs, out):
@@ -42,30 +43,27 @@ def tile_picked_haar_gelu_e_kernel(tc, xT, w1, w2_words, w2_scales, w3_words, w3
         nc.vector.memset(warm_in[:], 0.0)
         nc.scalar.activation(warm_out[:], warm_in[:], GELU)
 
-        band_scales = []
-        for name, scales in (("w2", w2_scales), ("w3", w3_scales)):
-            plane = sbuf(name + "_plane", [P, N], U8)
-            nc.gpsimd.memset(plane[:], 0)
-            for q in range(4):
-                nc.gpsimd.dma_start(out=plane[32 * q : 32 * q + 4, :].bitcast(I32), in_=scales[0, 4 * q : 4 * q + 4, :].bitcast(I32))
-            band_scales.append(plane)
+        band_plane = sbuf("band_plane", [P, 2, N], U8)
+        nc.vector.memset(band_plane[:].rearrange("p b n -> p (b n)").bitcast(I32), 0)
 
-        x_rows = xT.rearrange("(z p j) t -> z j p t", z=2, j=PACK)
+        x_rows = xT.rearrange("(z p j) t -> z p j t", z=2, j=PACK)
         w_rows = w1.rearrange("(z p j) c -> z p j c", z=2, j=PACK)
         planes = {}
 
-        def load_plane(z, j):
-            planes[z, j] = sbuf("x_%d_%d" % (z, j), [P, T], F32)
-            nc.sync.dma_start(out=planes[z, j][:], in_=x_rows[z, j])
+        def load_planes(z, first, count):
+            tile = sbuf("x_%d_%d" % (z, first), [P, count, T], F32)
+            nc.sync.dma_start(out=tile[:], in_=x_rows[z][:, first : first + count, :])
+            for j in range(count):
+                planes[z, first + j] = tile[:, j, :]
 
-        load_plane(0, 0)
+        load_planes(0, 0, 2)
         nc.sync.dma_start(offsets[:], offs)
+        load_planes(0, 2, 2)
+        load_planes(1, 0, 2)
         w_first = sbuf("w_first", [P, PACK, H], F32)
         nc.sync.dma_start(out=w_first[:], in_=w_rows[0])
-        for z in range(2):
-            for j in range(PACK):
-                if (z, j) != (0, 0):
-                    load_plane(z, j)
+        load_planes(1, 2, 1)
+        load_planes(1, 3, 1)
         w_last = []
         for half in range(2):
             raw = sbuf("w_last_%d" % half, [P, PACK, H // 2], F32)
@@ -76,6 +74,11 @@ def tile_picked_haar_gelu_e_kernel(tc, xT, w1, w2_words, w2_scales, w3_words, w3
             tile = sbuf(name + "_codes", [P, N], I32)
             nc.sync.dma_start(out=tile[:], in_=words[0].rearrange("p n r -> p (n r)").bitcast(I32))
             band_words.append(tile)
+        for b, scales in enumerate((w2_scales, w3_scales)):
+            for q in range(4):
+                nc.sync.dma_start(
+                    out=band_plane[32 * q : 32 * q + 4, b, :].bitcast(I32), in_=scales[0, 4 * q : 4 * q + 4, :].bitcast(I32)
+                )
 
         w_codes = [sbuf("w_codes_%d" % z, [P, H], U32) for z in range(2)]
         w_scales = [sbuf("w_scales_%d" % z, [P, H], U8) for z in range(2)]
@@ -83,93 +86,101 @@ def tile_picked_haar_gelu_e_kernel(tc, xT, w1, w2_words, w2_scales, w3_words, w3
         x_scales = {}
         picked = [sbuf("picked_%d" % z, [P, S, PACK], BF16) for z in range(2)]
 
-        def gather(z):
-            for j in range(PACK):
-                nc.vector.tensor_copy(
-                    out=picked[z][:, :, j].rearrange("p (g d v) -> p d g v", g=GROUPS, d=2),
-                    in_=planes[z, j][:].indirect(offsets[:]),
-                )
+        def gather(z, j):
+            nc.vector.tensor_copy(
+                out=picked[z][:, :, j].rearrange("p (g d v) -> p d g v", g=GROUPS, d=2),
+                in_=planes[z, j].indirect(offsets[:]),
+            )
 
-        def quantize_picked(z, half):
-            x_codes[z, half] = sbuf("x_codes_%d_%d" % (z, half), [P, S // 2], U32)
-            x_scales[z, half] = sbuf("x_scales_%d_%d" % (z, half), [P, S // 2], U8)
-            values = picked[z][:, half * (S // 2) : (half + 1) * (S // 2), :].rearrange("p s j -> p (s j)")
-            quantize(x_codes[z, half][:], x_scales[z, half][:], values)
+        def quantize_picked(z, first, count):
+            codes = sbuf("x_codes_%d_%d" % (z, first), [P, count * P], U32)
+            scales = sbuf("x_scales_%d_%d" % (z, first), [P, count * P], U8)
+            quantize(codes[:], scales[:], picked[z][:, first * P : (first + count) * P, :].rearrange("p s j -> p (s j)"))
+            for g in range(count):
+                x_codes[z, first + g] = codes[:, g * P : (g + 1) * P]
+                x_scales[z, first + g] = scales[:, g * P : (g + 1) * P]
 
         hidden = [ps.tile([P, PACK, P], F32, name="hidden_%d" % g) for g in range(GROUPS)]
 
         def first_product(z, g):
-            cols = slice((g % 2) * P, (g % 2 + 1) * P)
             for t in range(PACK):
                 nc.tensor.matmul_mx(
                     out=hidden[g][:, t, :],
                     lhsT=w_codes[z][:, t * P : (t + 1) * P].bitcast(FP8X4),
                     lhsT_scale=w_scales[z][:, t * P : (t + 1) * P],
-                    rhs=x_codes[z, g // 2][:, cols].bitcast(FP8X4),
-                    rhs_scale=x_scales[z, g // 2][:, cols],
+                    rhs=x_codes[z, g].bitcast(FP8X4),
+                    rhs_scale=x_scales[z, g],
                     start=(z == 0 and t == 0),
                     stop=(z == 1 and t == PACK - 1),
                 )
 
+        def deal(engine_copy, target, source, lo, hi):
+            engine_copy(
+                out=target[:, :, lo:hi, :].rearrange("p t m j -> p m j t"),
+                in_=source[:].rearrange("p j (m t) -> p m j t", t=PACK)[:, lo:hi],
+            )
+
+        for j in range(PACK):
+            gather(0, j)
+        quantize_picked(0, 0, GROUPS)
+        for j in range(PACK - 1):
+            gather(1, j)
         w_bf = sbuf("w_bf", [P, PACK, P, PACK], BF16)
-        nc.scalar.copy(out=w_bf[:].rearrange("p t m j -> p m j t"), in_=w_first[:].rearrange("p j (m t) -> p m j t", t=PACK))
+        deal(nc.scalar.copy, w_bf, w_first, 0, P)
         quantize(w_codes[0][:], w_scales[0][:], w_bf[:].rearrange("p t m j -> p (t m j)"))
-        gather(0)
-        for half in range(2):
-            quantize_picked(0, half)
         for g in range(GROUPS):
             first_product(0, g)
 
-        gather(1)
-        quantize_picked(1, 0)
+        gather(1, PACK - 1)
+        quantize_picked(1, 0, 1)
         for half in range(2):
-            for pair in range(2):
-                piece = sbuf("w_bf_%d_%d" % (half, pair), [P, 2, P // 2, PACK], BF16)
-                source = w_last[half][:].rearrange("p j (m t) -> p m j t", t=PACK)[:, :, :, 2 * pair : 2 * pair + 2]
-                target = piece[:].rearrange("p t m j -> p m j t")
-                if half == 1 and pair == 0:
-                    nc.vector.tensor_copy(out=target, in_=source)
-                else:
-                    nc.scalar.copy(out=target, in_=source)
-                for u in range(2):
-                    first = (2 * pair + u) * P + half * (P // 2)
-                    cols = slice(first, first + P // 2)
-                    quantize(w_codes[1][:, cols], w_scales[1][:, cols], piece[:, u].rearrange("p m j -> p (m j)"))
-        quantize_picked(1, 1)
+            piece = sbuf("w_bf_%d" % half, [P, PACK, P // 2, PACK], BF16)
+            if half == 0:
+                deal(nc.scalar.copy, piece, w_last[half], 0, P // 2)
+            else:
+                deal(nc.vector.tensor_copy, piece, w_last[half], 0, VECTOR_SHARE)
+                deal(nc.scalar.copy, piece, w_last[half], VECTOR_SHARE, P // 2)
+            for t in range(PACK):
+                cols = slice(t * P + half * (P // 2), t * P + (half + 1) * (P // 2))
+                quantize(w_codes[1][:, cols], w_scales[1][:, cols], piece[:, t].rearrange("p m j -> p (m j)"))
+        quantize_picked(1, 1, 1)
+        quantize_picked(1, 2, 2)
 
         out_rows = out.rearrange("(a p) v -> p a v", p=P)
         for half in range(2):
-            codes = [sbuf("band_codes_%d_%d" % (half, b), [P, P], U32) for b in range(2)]
-            scales = [sbuf("band_scales_%d_%d" % (half, b), [P, P], U8) for b in range(2)]
+            bands = [sbuf("band_%d_%d" % (half, b), [P, 2, PAIRS * PACK], BF16) for b in range(2)]
             for g in range(2 * half, 2 * half + 2):
                 first_product(1, g)
                 h = sbuf("h_%d" % g, [P, 2, PAIRS * PACK], F32)
                 nc.scalar.activation(
                     h[:].rearrange("p d (v t) -> p (d v) t", t=PACK), hidden[g][:].rearrange("p t n -> p n t"), GELU
                 )
-                bands = [sbuf("band_%d_%d" % (g, b), [P, PAIRS * PACK], BF16) for b in range(2)]
                 for b, op in enumerate((ADD, SUB)):
-                    nc.vector.tensor_tensor(bands[b][:], h[:, 0, :], h[:, 1, :], op)
-                cols = slice((g % 2) * PAIRS, (g % 2 + 1) * PAIRS)
-                for b in range(2):
-                    quantize(codes[b][:, cols], scales[b][:, cols], bands[b][:])
-            for a in range(2):
-                acc = ps.tile([P, P], F32, name="acc_%d_%d" % (half, a))
-                for b in range(2):
+                    nc.vector.tensor_tensor(bands[b][:, g % 2, :], h[:, 0, :], h[:, 1, :], op)
+            acc = [ps.tile([P, P], F32, name="acc_%d_%d" % (half, a)) for a in range(2)]
+            for b in range(2):
+                codes = sbuf("band_codes_%d_%d" % (half, b), [P, P], U32)
+                scales = sbuf("band_scales_%d_%d" % (half, b), [P, P], U8)
+                quantize(codes[:], scales[:], bands[b][:].rearrange("p g e -> p (g e)"))
+                for a in range(2):
                     nc.tensor.matmul_mx(
-                        out=acc[:],
+                        out=acc[a][:],
                         lhsT=band_words[b][:, a * P : (a + 1) * P].bitcast(FP8X4),
-                        lhsT_scale=band_scales[b][:, a * P : (a + 1) * P],
-                        rhs=codes[b][:].bitcast(FP8X4),
-                        rhs_scale=scales[b][:],
+                        lhsT_scale=band_plane[:, b, a * P : (a + 1) * P],
+                        rhs=codes[:].bitcast(FP8X4),
+                        rhs_scale=scales[:],
                         start=(b == 0),
                         stop=(b == 1),
                     )
-                result = sbuf("result_%d_%d" % (half, a), [P, P], F32)
-                if half == 1 and a == 1:
-                    nc.vector.tensor_scalar_mul(result[:], acc[:], 0.5)
-                    nc.sync.dma_start(out=out_rows[:, a, half * P : (half + 1) * P], in_=result[:])
-                else:
-                    nc.scalar.mul(result[:], acc[:], 0.5)
-                    queue = nc.scalar if half == 1 else nc.sync
-                    queue.dma_start(out=out_rows[:, a, half * P : (half + 1) * P], in_=result[:])
+            cols = slice(half * P, (half + 1) * P)
+            if half == 0:
+                result = sbuf("result_0", [P, 2, P], F32)
+                for a in range(2):
+                    nc.scalar.mul(result[:, a, :], acc[a][:], 0.5)
+                nc.sync.dma_start(out=out_rows[:, :, cols], in_=result[:])
+            else:
+                results = [sbuf("result_1_%d" % a, [P, P], F32) for a in range(2)]
+                nc.scalar.mul(results[0][:], acc[0][:], 0.5)
+                nc.scalar.dma_start(out=out_rows[:, 0, cols], in_=results[0][:])
+                nc.vector.tensor_scalar_mul(results[1][:], acc[1][:], 0.5)
+                nc.sync.dma_start(out=out_rows[:, 1, cols], in_=results[1][:])

@@ -21,7 +21,6 @@ PACK = 4
 K_PASS = P * PACK
 GROUPS = 4
 PAIRS = V // GROUPS
-VECTOR_SHARE = 40
 
 
 def tile_picked_haar_gelu_e_kernel(tc, xT, w1, w2_words, w2_scales, w3_words, w3_scales, offs, out):
@@ -30,8 +29,8 @@ def tile_picked_haar_gelu_e_kernel(tc, xT, w1, w2_words, w2_scales, w3_words, w3
         sb = ctx.enter_context(tc.tile_pool(name="sb", bufs=1))
         ps = ctx.enter_context(tc.psum_pool(name="ps", bufs=1))
 
-        def sbuf(name, shape, dtype):
-            return sb.tile(shape, dtype, name=name, align_bytes=64)
+        def sbuf(name, shape, dtype, tag=None):
+            return sb.tile(shape, dtype, name=name, tag=tag or name, align_bytes=64)
 
         def quantize(codes, scales, values):
             nc.vector.quantize_mx(out=codes.bitcast(FP8X4), scales=scales, in_=values)
@@ -65,9 +64,9 @@ def tile_picked_haar_gelu_e_kernel(tc, xT, w1, w2_words, w2_scales, w3_words, w3
         load_planes(1, 2, 1)
         load_planes(1, 3, 1)
         w_last = []
-        for half in range(2):
-            raw = sbuf("w_last_%d" % half, [P, PACK, H // 2], F32)
-            nc.sync.dma_start(out=raw[:], in_=w_rows[1][:, :, half * (H // 2) : (half + 1) * (H // 2)])
+        for quarter in range(4):
+            raw = sbuf("w_last_%d" % quarter, [P, PACK, H // 4], F32)
+            nc.sync.dma_start(out=raw[:], in_=w_rows[1][:, :, quarter * (H // 4) : (quarter + 1) * (H // 4)])
             w_last.append(raw)
         band_words = []
         for name, words in (("w2", w2_words), ("w3", w3_words)):
@@ -80,7 +79,7 @@ def tile_picked_haar_gelu_e_kernel(tc, xT, w1, w2_words, w2_scales, w3_words, w3
                     out=band_plane[32 * q : 32 * q + 4, b, :].bitcast(I32), in_=scales[0, 4 * q : 4 * q + 4, :].bitcast(I32)
                 )
 
-        w_codes = [sbuf("w_codes_%d" % z, [P, H], U32) for z in range(2)]
+        w_codes = [None, sbuf("w_codes_1", [P, H], U32)]
         w_scales = [sbuf("w_scales_%d" % z, [P, H], U8) for z in range(2)]
         x_codes = {}
         x_scales = {}
@@ -92,10 +91,11 @@ def tile_picked_haar_gelu_e_kernel(tc, xT, w1, w2_words, w2_scales, w3_words, w3
                 in_=planes[z, j].indirect(offsets[:]),
             )
 
-        def quantize_picked(z, first, count):
-            codes = sbuf("x_codes_%d_%d" % (z, first), [P, count * P], U32)
+        def quantize_picked(z, first, count, codes=None):
+            if codes is None:
+                codes = sbuf("x_codes_%d_%d" % (z, first), [P, count * P], U32)[:]
             scales = sbuf("x_scales_%d_%d" % (z, first), [P, count * P], U8)
-            quantize(codes[:], scales[:], picked[z][:, first * P : (first + count) * P, :].rearrange("p s j -> p (s j)"))
+            quantize(codes, scales[:], picked[z][:, first * P : (first + count) * P, :].rearrange("p s j -> p (s j)"))
             for g in range(count):
                 x_codes[z, first + g] = codes[:, g * P : (g + 1) * P]
                 x_scales[z, first + g] = scales[:, g * P : (g + 1) * P]
@@ -114,11 +114,11 @@ def tile_picked_haar_gelu_e_kernel(tc, xT, w1, w2_words, w2_scales, w3_words, w3
                     stop=(z == 1 and t == PACK - 1),
                 )
 
-        def deal(engine_copy, target, source, lo, hi):
-            engine_copy(
-                out=target[:, :, lo:hi, :].rearrange("p t m j -> p m j t"),
-                in_=source[:].rearrange("p j (m t) -> p m j t", t=PACK)[:, lo:hi],
-            )
+        def deal(engine_copy, target, source):
+            engine_copy(out=target.rearrange("p t m j -> p m j t"), in_=source)
+
+        def by_channel(raw):
+            return raw[:].rearrange("p j (m t) -> p m j t", t=PACK)
 
         for j in range(PACK):
             gather(0, j)
@@ -126,25 +126,33 @@ def tile_picked_haar_gelu_e_kernel(tc, xT, w1, w2_words, w2_scales, w3_words, w3
         for j in range(PACK - 1):
             gather(1, j)
         w_bf = sbuf("w_bf", [P, PACK, P, PACK], BF16)
-        deal(nc.scalar.copy, w_bf, w_first, 0, P)
+        deal(nc.scalar.copy, w_bf[:], by_channel(w_first))
+        w_codes[0] = sbuf("w_codes_0", [P, H], U32, "x_1_2")
         quantize(w_codes[0][:], w_scales[0][:], w_bf[:].rearrange("p t m j -> p (t m j)"))
         for g in range(GROUPS):
             first_product(0, g)
 
         gather(1, PACK - 1)
         quantize_picked(1, 0, 1)
-        for half in range(2):
-            piece = sbuf("w_bf_%d" % half, [P, PACK, P // 2, PACK], BF16)
-            if half == 0:
-                deal(nc.scalar.copy, piece, w_last[half], 0, P // 2)
-            else:
-                deal(nc.vector.tensor_copy, piece, w_last[half], 0, VECTOR_SHARE)
-                deal(nc.scalar.copy, piece, w_last[half], VECTOR_SHARE, P // 2)
-            for t in range(PACK):
-                cols = slice(t * P + half * (P // 2), t * P + (half + 1) * (P // 2))
-                quantize(w_codes[1][:, cols], w_scales[1][:, cols], piece[:, t].rearrange("p m j -> p (m j)"))
-        quantize_picked(1, 1, 1)
-        quantize_picked(1, 2, 2)
+        def quantize_w_last(half, t, values):
+            cols = slice(t * P + half * (P // 2), t * P + (half + 1) * (P // 2))
+            quantize(w_codes[1][:, cols], w_scales[1][:, cols], values.rearrange("p m j -> p (m j)"))
+
+        early = sbuf("w_bf_early", [P, PACK, P // 2, PACK], BF16)
+        for quarter in range(2):
+            deal(nc.scalar.copy, early[:, :, quarter * 32 : (quarter + 1) * 32, :], by_channel(w_last[quarter]))
+        for t in range(PACK):
+            quantize_w_last(0, t, early[:, t])
+        late = [sbuf("w_bf_late_%d" % pair, [P, 2, P // 2, PACK], BF16) for pair in range(2)]
+        for pair in range(2):
+            deal(nc.scalar.copy, late[pair][:, :, 0:32, :], by_channel(w_last[2])[:, :, :, 2 * pair : 2 * pair + 2])
+        for pair, engine_copy in enumerate((nc.vector.tensor_copy, nc.scalar.copy)):
+            deal(engine_copy, late[pair][:, :, 32:64, :], by_channel(w_last[3])[:, :, :, 2 * pair : 2 * pair + 2])
+        for t in range(PACK):
+            quantize_w_last(1, t, late[t // 2][:, t % 2])
+        held = sbuf("x_codes_held", [P, 3 * P], U32, "w_bf_late_1")
+        quantize_picked(1, 1, 1, held[:, 0:P])
+        quantize_picked(1, 2, 2, held[:, P : 3 * P])
 
         out_rows = out.rearrange("(a p) v -> p a v", p=P)
         for half in range(2):
@@ -153,7 +161,7 @@ def tile_picked_haar_gelu_e_kernel(tc, xT, w1, w2_words, w2_scales, w3_words, w3
                 first_product(1, g)
                 h = sbuf("h_%d" % g, [P, 2, PAIRS * PACK], F32)
                 nc.scalar.activation(
-                    h[:].rearrange("p d (v t) -> p (d v) t", t=PACK), hidden[g][:].rearrange("p t n -> p n t"), GELU
+                    h[:].rearrange("p d (v t) -> p (d v) t", t=PACK), hidden[g][:].rearrange("p t n -> p n t"), GELU, bias=warm_out[:]
                 )
                 for b, op in enumerate((ADD, SUB)):
                     nc.vector.tensor_tensor(bands[b][:, g % 2, :], h[:, 0, :], h[:, 1, :], op)

@@ -68,16 +68,16 @@ def tile_picked_haar_gelu_e_kernel(tc, xT, w1, w2_words, w2_scales, w3_words, w3
             raw = sbuf("w_last_%d" % quarter, [P, PACK, H // 4], F32)
             nc.sync.dma_start(out=raw[:], in_=w_rows[1][:, :, quarter * (H // 4) : (quarter + 1) * (H // 4)])
             w_last.append(raw)
-        band_words = []
-        for name, words in (("w2", w2_words), ("w3", w3_words)):
-            tile = sbuf(name + "_codes", [P, N], I32)
-            nc.sync.dma_start(out=tile[:], in_=words[0].rearrange("p n r -> p (n r)").bitcast(I32))
-            band_words.append(tile)
         for b, scales in enumerate((w2_scales, w3_scales)):
             for q in range(4):
                 nc.sync.dma_start(
                     out=band_plane[32 * q : 32 * q + 4, b, :].bitcast(I32), in_=scales[0, 4 * q : 4 * q + 4, :].bitcast(I32)
                 )
+        band_words = []
+        for name, words in (("w2", w2_words), ("w3", w3_words)):
+            tile = sbuf(name + "_codes", [P, N], I32)
+            nc.sync.dma_start(out=tile[:], in_=words[0].rearrange("p n r -> p (n r)").bitcast(I32))
+            band_words.append(tile)
 
         w_codes = [None, sbuf("w_codes_1", [P, H], U32)]
         w_scales = [sbuf("w_scales_%d" % z, [P, H], U8) for z in range(2)]
@@ -143,40 +143,50 @@ def tile_picked_haar_gelu_e_kernel(tc, xT, w1, w2_words, w2_scales, w3_words, w3
             deal(nc.scalar.copy, early[:, :, quarter * 32 : (quarter + 1) * 32, :], by_channel(w_last[quarter]))
         for t in range(PACK):
             quantize_w_last(0, t, early[:, t])
-        late = [sbuf("w_bf_late_%d" % pair, [P, 2, P // 2, PACK], BF16) for pair in range(2)]
+        late = sbuf("w_bf_late", [P, PACK, P // 2, PACK], BF16)
+        deal(nc.scalar.copy, late[:, :, 0:32, :], by_channel(w_last[2]))
         for pair in range(2):
-            deal(nc.scalar.copy, late[pair][:, :, 0:32, :], by_channel(w_last[2])[:, :, :, 2 * pair : 2 * pair + 2])
-        for pair, engine_copy in enumerate((nc.vector.tensor_copy, nc.scalar.copy)):
-            deal(engine_copy, late[pair][:, :, 32:64, :], by_channel(w_last[3])[:, :, :, 2 * pair : 2 * pair + 2])
+            slots = slice(2 * pair, 2 * pair + 2)
+            deal(nc.vector.tensor_copy, late[:, slots, 32:64, :], by_channel(w_last[3])[:, :, :, slots])
         for t in range(PACK):
-            quantize_w_last(1, t, late[t // 2][:, t % 2])
-        held = sbuf("x_codes_held", [P, 3 * P], U32, "w_bf_late_1")
+            quantize_w_last(1, t, late[:, t])
+        held = sbuf("x_codes_held", [P, 3 * P], U32, "w_bf_late")
         quantize_picked(1, 1, 1, held[:, 0:P])
         quantize_picked(1, 2, 2, held[:, P : 3 * P])
 
         out_rows = out.rearrange("(a p) v -> p a v", p=P)
         for half in range(2):
             bands = [sbuf("band_%d_%d" % (half, b), [P, 2, PAIRS * PACK], BF16) for b in range(2)]
+            codes = [sbuf("band_codes_%d_%d" % (half, b), [P, P], U32) for b in range(2)]
+            scales = [sbuf("band_scales_%d_%d" % (half, b), [P, P], U8) for b in range(2)]
             for g in range(2 * half, 2 * half + 2):
                 first_product(1, g)
-                h = sbuf("h_%d" % g, [P, 2, PAIRS * PACK], F32)
-                nc.scalar.activation(
-                    h[:].rearrange("p d (v t) -> p (d v) t", t=PACK), hidden[g][:].rearrange("p t n -> p n t"), GELU, bias=warm_out[:]
-                )
-                for b, op in enumerate((ADD, SUB)):
-                    nc.vector.tensor_tensor(bands[b][:, g % 2, :], h[:, 0, :], h[:, 1, :], op)
+                stretches = ((0, PAIRS // 2), (PAIRS // 2, PAIRS)) if g == 0 else ((0, PAIRS),)
+                for first, last in stretches:
+                    h = sbuf("h_%d_%d" % (g, first), [P, 2, (last - first) * PACK], F32)
+                    nc.scalar.activation(
+                        h[:].rearrange("p d (v t) -> p d v t", t=PACK),
+                        hidden[g][:].rearrange("p t (d v) -> p d v t", d=2)[:, :, first:last, :],
+                        GELU,
+                        bias=warm_out[:],
+                    )
+                    for b, op in enumerate((ADD, SUB)):
+                        nc.vector.tensor_tensor(bands[b][:, g % 2, first * PACK : last * PACK], h[:, 0, :], h[:, 1, :], op)
+                if half == 0:
+                    for b in range(2):
+                        cols = slice(g * PAIRS, (g + 1) * PAIRS)
+                        quantize(codes[b][:, cols], scales[b][:, cols], bands[b][:, g, :])
             acc = [ps.tile([P, P], F32, name="acc_%d_%d" % (half, a)) for a in range(2)]
             for b in range(2):
-                codes = sbuf("band_codes_%d_%d" % (half, b), [P, P], U32)
-                scales = sbuf("band_scales_%d_%d" % (half, b), [P, P], U8)
-                quantize(codes[:], scales[:], bands[b][:].rearrange("p g e -> p (g e)"))
+                if half == 1:
+                    quantize(codes[b][:], scales[b][:], bands[b][:].rearrange("p g e -> p (g e)"))
                 for a in range(2):
                     nc.tensor.matmul_mx(
                         out=acc[a][:],
                         lhsT=band_words[b][:, a * P : (a + 1) * P].bitcast(FP8X4),
                         lhsT_scale=band_plane[:, b, a * P : (a + 1) * P],
-                        rhs=codes[:].bitcast(FP8X4),
-                        rhs_scale=scales[:],
+                        rhs=codes[b][:].bitcast(FP8X4),
+                        rhs_scale=scales[b][:],
                         start=(b == 0),
                         stop=(b == 1),
                     )

@@ -176,7 +176,7 @@ def tile_picked_haar_gelu_e_kernel(tc, xT, w1, w2_words, w2_scales, w3_words, w3
                     for b in range(2):
                         cols = slice(g * PAIRS, (g + 1) * PAIRS)
                         quantize(codes[b][:, cols], scales[b][:, cols], bands[b][:, g, :])
-            acc = [ps.tile([P, P], F32, name="acc_%d_%d" % (half, a)) for a in range(2)]
+            acc = [ps.tile([P, P], F32, name="acc_%d_%d" % (half, a), tag="acc_%d" % a) for a in range(2)]
             for b in range(2):
                 if half == 1:
                     quantize(codes[b][:], scales[b][:], bands[b][:].rearrange("p g e -> p (g e)"))

@@ -161,7 +161,7 @@ def tile_picked_haar_gelu_e_kernel(tc, xT, w1, w2_words, w2_scales, w3_words, w3
             scales = [sbuf("band_scales_%d_%d" % (half, b), [P, P], U8) for b in range(2)]
             for g in range(2 * half, 2 * half + 2):
                 first_product(1, g)
-                stretches = ((0, PAIRS // 2), (PAIRS // 2, PAIRS)) if g == 0 else ((0, PAIRS),)
+                stretches = ((0, PAIRS // 2), (PAIRS // 2, PAIRS)) if g < 3 else ((0, PAIRS),)
                 for first, last in stretches:
                     h = sbuf("h_%d_%d" % (g, first), [P, 2, (last - first) * PACK], F32)
                     nc.scalar.activation(
@@ -172,14 +172,9 @@ def tile_picked_haar_gelu_e_kernel(tc, xT, w1, w2_words, w2_scales, w3_words, w3
                     )
                     for b, op in enumerate((ADD, SUB)):
                         nc.vector.tensor_tensor(bands[b][:, g % 2, first * PACK : last * PACK], h[:, 0, :], h[:, 1, :], op)
-                if half == 0:
-                    for b in range(2):
-                        cols = slice(g * PAIRS, (g + 1) * PAIRS)
-                        quantize(codes[b][:, cols], scales[b][:, cols], bands[b][:, g, :])
             acc = [ps.tile([P, P], F32, name="acc_%d_%d" % (half, a), tag="acc_%d" % a) for a in range(2)]
             for b in range(2):
-                if half == 1:
-                    quantize(codes[b][:], scales[b][:], bands[b][:].rearrange("p g e -> p (g e)"))
+                quantize(codes[b][:], scales[b][:], bands[b][:].rearrange("p g e -> p (g e)"))
                 for a in range(2):
                     nc.tensor.matmul_mx(
                         out=acc[a][:],

@@ -63,11 +63,8 @@ def tile_picked_haar_gelu_e_kernel(tc, xT, w1, w2_words, w2_scales, w3_words, w3
         nc.sync.dma_start(out=w_first[:], in_=w_rows[0])
         load_planes(1, 2, 1)
         load_planes(1, 3, 1)
-        w_last = []
-        for quarter in range(4):
-            raw = sbuf("w_last_%d" % quarter, [P, PACK, H // 4], F32)
-            nc.sync.dma_start(out=raw[:], in_=w_rows[1][:, :, quarter * (H // 4) : (quarter + 1) * (H // 4)])
-            w_last.append(raw)
+        w_last = sbuf("w_last", [P, PACK, H], F32)
+        nc.sync.dma_start(out=w_last[:], in_=w_rows[1])
         for b, scales in enumerate((w2_scales, w3_scales)):
             for q in range(4):
                 nc.sync.dma_start(
@@ -81,6 +78,8 @@ def tile_picked_haar_gelu_e_kernel(tc, xT, w1, w2_words, w2_scales, w3_words, w3
 
         w_codes = [None, sbuf("w_codes_1", [P, H], U32)]
         w_scales = [sbuf("w_scales_%d" % z, [P, H], U8) for z in range(2)]
+        slot_codes = {1: [w_codes[1][:, t * P : (t + 1) * P] for t in range(PACK)]}
+        slot_scales = {1: [w_scales[1][:, t * P : (t + 1) * P] for t in range(PACK)]}
         x_codes = {}
         x_scales = {}
         picked = [sbuf("picked_%d" % z, [P, S, PACK], BF16) for z in range(2)]
@@ -102,15 +101,15 @@ def tile_picked_haar_gelu_e_kernel(tc, xT, w1, w2_words, w2_scales, w3_words, w3
 
         hidden = [ps.tile([P, PACK, P], F32, name="hidden_%d" % g) for g in range(GROUPS)]
 
-        def first_product(z, g):
-            for t in range(PACK):
+        def first_product(z, g, slots=(0, 1, 2, 3)):
+            for t in slots:
                 nc.tensor.matmul_mx(
                     out=hidden[g][:, t, :],
-                    lhsT=w_codes[z][:, t * P : (t + 1) * P].bitcast(FP8X4),
-                    lhsT_scale=w_scales[z][:, t * P : (t + 1) * P],
+                    lhsT=slot_codes[z][t].bitcast(FP8X4),
+                    lhsT_scale=slot_scales[z][t],
                     rhs=x_codes[z, g].bitcast(FP8X4),
                     rhs_scale=x_scales[z, g],
-                    start=(z == 0 and t == 0),
+                    start=(z == 0 and t == (0 if g < 2 else 3)),
                     stop=(z == 1 and t == PACK - 1),
                 )
 
@@ -123,36 +122,40 @@ def tile_picked_haar_gelu_e_kernel(tc, xT, w1, w2_words, w2_scales, w3_words, w3
         for j in range(PACK):
             gather(0, j)
         quantize_picked(0, 0, GROUPS)
-        for j in range(PACK - 1):
+        for j in range(2):
             gather(1, j)
         w_bf = sbuf("w_bf", [P, PACK, P, PACK], BF16)
-        deal(nc.scalar.copy, w_bf[:], by_channel(w_first))
-        w_codes[0] = sbuf("w_codes_0", [P, H], U32, "x_1_2")
-        quantize(w_codes[0][:], w_scales[0][:], w_bf[:].rearrange("p t m j -> p (t m j)"))
-        for g in range(GROUPS):
-            first_product(0, g)
+        deal(nc.scalar.copy, w_bf[:, :, 0:80, :], by_channel(w_first)[:, 0:80])
+        deal(nc.vector.tensor_copy, w_bf[:, :, 80:P, :], by_channel(w_first)[:, 80:P])
+        first_codes = sbuf("w_codes_0", [P, 2 * P], U32)
+        quantize(first_codes[:], w_scales[0][:, P : 3 * P], w_bf[:, 1:3].rearrange("p t m j -> p (t m j)"))
+        held = {}
+        for t, j in ((0, 2), (3, 3)):
+            gather(1, j)
+            held_codes = sbuf("w_codes_0_%d" % t, [P, P], U32, "x_1_%d" % j)
+            held_scales = sbuf("w_scales_0_%d" % t, [P, P], U8)
+            quantize(held_codes[:], held_scales[:], w_bf[:, t].rearrange("p m j -> p (m j)"))
+            held[t] = (held_codes[:], held_scales[:])
+        slot_codes[0] = [held[0][0], first_codes[:, 0:P], first_codes[:, P : 2 * P], held[3][0]]
+        slot_scales[0] = [held[0][1], w_scales[0][:, P : 2 * P], w_scales[0][:, 2 * P : 3 * P], held[3][1]]
+        for g in range(2):
+            first_product(0, g, (0, 1, 2))
+        for g in range(2):
+            first_product(0, g, (3,))
+        for g in range(2, GROUPS):
+            first_product(0, g, (3, 0, 1, 2))
 
-        gather(1, PACK - 1)
         quantize_picked(1, 0, 1)
-        def quantize_w_last(half, t, values):
-            cols = slice(t * P + half * (P // 2), t * P + (half + 1) * (P // 2))
-            quantize(w_codes[1][:, cols], w_scales[1][:, cols], values.rearrange("p m j -> p (m j)"))
-
-        early = sbuf("w_bf_early", [P, PACK, P // 2, PACK], BF16)
-        for quarter in range(2):
-            deal(nc.scalar.copy, early[:, :, quarter * 32 : (quarter + 1) * 32, :], by_channel(w_last[quarter]))
-        for t in range(PACK):
-            quantize_w_last(0, t, early[:, t])
-        late = sbuf("w_bf_late", [P, PACK, P // 2, PACK], BF16)
-        deal(nc.scalar.copy, late[:, :, 0:32, :], by_channel(w_last[2]))
+        late = sbuf("w_bf_late", [P, PACK, P, PACK], BF16)
         for pair in range(2):
             slots = slice(2 * pair, 2 * pair + 2)
-            deal(nc.vector.tensor_copy, late[:, slots, 32:64, :], by_channel(w_last[3])[:, :, :, slots])
+            deal(nc.vector.tensor_copy, late[:, slots, 0:80, :], by_channel(w_last)[:, 0:80, :, slots])
+            deal(nc.scalar.copy, late[:, slots, 80:P, :], by_channel(w_last)[:, 80:P, :, slots])
         for t in range(PACK):
-            quantize_w_last(1, t, late[:, t])
-        held = sbuf("x_codes_held", [P, 3 * P], U32, "w_bf_late")
-        quantize_picked(1, 1, 1, held[:, 0:P])
-        quantize_picked(1, 2, 2, held[:, P : 3 * P])
+            quantize(slot_codes[1][t], slot_scales[1][t], late[:, t].rearrange("p m j -> p (m j)"))
+        late_codes = sbuf("x_codes_held", [P, 3 * P], U32, "w_bf_late")
+        quantize_picked(1, 1, 1, late_codes[:, 0:P])
+        quantize_picked(1, 2, 2, late_codes[:, P : 3 * P])
 
         out_rows = out.rearrange("(a p) v -> p a v", p=P)
         for half in range(2):

@@ -13,6 +13,7 @@ U16 = mybir.dt.uint16
 U8 = mybir.dt.uint8
 FP8X4 = mybir.dt.float8_e4m3fn_x4
 GELU = mybir.ActivationFunctionType.Gelu_apprx_tanh
+COPY = mybir.ActivationFunctionType.Copy
 ADD = mybir.AluOpType.add
 SUB = mybir.AluOpType.subtract
 
@@ -55,16 +56,14 @@ def tile_picked_haar_gelu_e_kernel(tc, xT, w1, w2_words, w2_scales, w3_words, w3
             for j in range(count):
                 planes[z, first + j] = tile[:, j, :]
 
-        load_planes(0, 0, 2)
+        load_planes(0, 0, 4)
         nc.sync.dma_start(offsets[:], offs)
-        load_planes(0, 2, 2)
         load_planes(1, 0, 2)
-        w_first = sbuf("w_first", [P, PACK, H], F32)
-        nc.sync.dma_start(out=w_first[:], in_=w_rows[0])
+        w_raw = [sbuf("w_raw_%d" % z, [P, PACK, H], F32) for z in range(2)]
+        nc.sync.dma_start(out=w_raw[0][:], in_=w_rows[0])
         load_planes(1, 2, 1)
         load_planes(1, 3, 1)
-        w_last = sbuf("w_last", [P, PACK, H], F32)
-        nc.sync.dma_start(out=w_last[:], in_=w_rows[1])
+        nc.sync.dma_start(out=w_raw[1][:], in_=w_rows[1])
         for b, scales in enumerate((w2_scales, w3_scales)):
             for q in range(4):
                 nc.sync.dma_start(
@@ -76,18 +75,19 @@ def tile_picked_haar_gelu_e_kernel(tc, xT, w1, w2_words, w2_scales, w3_words, w3
             nc.sync.dma_start(out=tile[:], in_=words[0].rearrange("p n r -> p (n r)").bitcast(I32))
             band_words.append(tile)
 
-        w_codes = [None, sbuf("w_codes_1", [P, H], U32)]
-        w_scales = [sbuf("w_scales_%d" % z, [P, H], U8) for z in range(2)]
-        slot_codes = {1: [w_codes[1][:, t * P : (t + 1) * P] for t in range(PACK)]}
-        slot_scales = {1: [w_scales[1][:, t * P : (t + 1) * P] for t in range(PACK)]}
-        x_codes = {}
-        x_scales = {}
+        slot_codes, slot_scales, x_codes, x_scales = {}, {}, {}, {}
         picked = [sbuf("picked_%d" % z, [P, S, PACK], BF16) for z in range(2)]
 
-        def gather(z, j):
-            nc.vector.tensor_copy(
-                out=picked[z][:, :, j].rearrange("p (g d v) -> p d g v", g=GROUPS, d=2),
-                in_=planes[z, j].indirect(offsets[:]),
+        def gather_pair(z, u):
+            pair = sbuf("pair_%d_%d" % (z, u), [P, 2, S], F32)
+            nc.scalar.activation(pair[:, 0, :], planes[z, 2 * u].indirect(offsets[:]), COPY)
+            nc.vector.tensor_copy(out=pair[:, 1, :], in_=planes[z, 2 * u + 1].indirect(offsets[:]))
+            return pair
+
+        def weave(engine_copy, z, u, pair, first, last):
+            engine_copy(
+                out=picked[z][:, :, 2 * u : 2 * u + 2].rearrange("p (g d v) e -> p g d v e", g=GROUPS, d=2)[:, first:last],
+                in_=pair[:].rearrange("p e (d g v) -> p g d v e", g=GROUPS, d=2)[:, first:last],
             )
 
         def quantize_picked(z, first, count, codes=None):
@@ -101,17 +101,16 @@ def tile_picked_haar_gelu_e_kernel(tc, xT, w1, w2_words, w2_scales, w3_words, w3
 
         hidden = [ps.tile([P, PACK, P], F32, name="hidden_%d" % g) for g in range(GROUPS)]
 
-        def first_product(z, g, slots=(0, 1, 2, 3)):
-            for t in slots:
-                nc.tensor.matmul_mx(
-                    out=hidden[g][:, t, :],
-                    lhsT=slot_codes[z][t].bitcast(FP8X4),
-                    lhsT_scale=slot_scales[z][t],
-                    rhs=x_codes[z, g].bitcast(FP8X4),
-                    rhs_scale=x_scales[z, g],
-                    start=(z == 0 and t == (0 if g < 2 else 3)),
-                    stop=(z == 1 and t == PACK - 1),
-                )
+        def first_product(z, g, t):
+            nc.tensor.matmul_mx(
+                out=hidden[g][:, t, :],
+                lhsT=slot_codes[z, t].bitcast(FP8X4),
+                lhsT_scale=slot_scales[z, t],
+                rhs=x_codes[z, g].bitcast(FP8X4),
+                rhs_scale=x_scales[z, g],
+                start=(z == 0 and t == 0),
+                stop=(z == 1 and t == PACK - 1),
+            )
 
         def deal(engine_copy, target, source):
             engine_copy(out=target.rearrange("p t m j -> p m j t"), in_=source)
@@ -119,40 +118,43 @@ def tile_picked_haar_gelu_e_kernel(tc, xT, w1, w2_words, w2_scales, w3_words, w3
         def by_channel(raw):
             return raw[:].rearrange("p j (m t) -> p m j t", t=PACK)
 
-        for j in range(PACK):
-            gather(0, j)
-        quantize_picked(0, 0, GROUPS)
-        for j in range(2):
-            gather(1, j)
-        w_bf = sbuf("w_bf", [P, PACK, P, PACK], BF16)
-        deal(nc.scalar.copy, w_bf[:, :, 0:80, :], by_channel(w_first)[:, 0:80])
-        deal(nc.vector.tensor_copy, w_bf[:, :, 80:P, :], by_channel(w_first)[:, 80:P])
-        first_codes = sbuf("w_codes_0", [P, 2 * P], U32)
-        quantize(first_codes[:], w_scales[0][:, P : 3 * P], w_bf[:, 1:3].rearrange("p t m j -> p (t m j)"))
-        held = {}
-        for t, j in ((0, 2), (3, 3)):
-            gather(1, j)
-            held_codes = sbuf("w_codes_0_%d" % t, [P, P], U32, "x_1_%d" % j)
-            held_scales = sbuf("w_scales_0_%d" % t, [P, P], U8)
-            quantize(held_codes[:], held_scales[:], w_bf[:, t].rearrange("p m j -> p (m j)"))
-            held[t] = (held_codes[:], held_scales[:])
-        slot_codes[0] = [held[0][0], first_codes[:, 0:P], first_codes[:, P : 2 * P], held[3][0]]
-        slot_scales[0] = [held[0][1], w_scales[0][:, P : 2 * P], w_scales[0][:, 2 * P : 3 * P], held[3][1]]
-        for g in range(2):
-            first_product(0, g, (0, 1, 2))
-        for g in range(2):
-            first_product(0, g, (3,))
-        for g in range(2, GROUPS):
-            first_product(0, g, (3, 0, 1, 2))
+        def quantize_slot(z, dealt, t, tag=None):
+            codes = sbuf("w_codes_%d_%d" % (z, t), [P, P], U32, tag)
+            scales = sbuf("w_scales_%d_%d" % (z, t), [P, P], U8)
+            quantize(codes[:], scales[:], dealt[:, t].rearrange("p m j -> p (m j)"))
+            slot_codes[z, t], slot_scales[z, t] = codes[:], scales[:]
 
+        for u in range(2):
+            weave(nc.vector.tensor_copy, 0, u, gather_pair(0, u), 0, GROUPS)
+        quantize_picked(0, 0, GROUPS)
+        weave(nc.vector.tensor_copy, 1, 0, gather_pair(1, 0), 0, GROUPS)
+
+        w_bf = sbuf("w_bf", [P, PACK, P, PACK], BF16)
+        deal(nc.vector.tensor_copy, w_bf[:, :, 0:80, :], by_channel(w_raw[0])[:, 0:80])
+        deal(nc.scalar.copy, w_bf[:, :, 80:P, :], by_channel(w_raw[0])[:, 80:P])
+        for t in range(1, PACK):
+            quantize_slot(0, w_bf, t)
+
+        last_pair = sbuf("pair_1_1", [P, 2, S], F32)
+        nc.scalar.activation(last_pair[:, 0, :], planes[1, 2].indirect(offsets[:]), COPY)
+        nc.vector.tensor_copy(out=last_pair[:, 1, 0:V], in_=planes[1, 3].indirect(offsets[:, 0 : V // 16]))
+        nc.scalar.activation(last_pair[:, 1, V:S], planes[1, 3].indirect(offsets[:, V // 16 : S // 16]), COPY)
+        quantize_slot(0, w_bf, 0, "x_1_3")
+        for t in range(PACK):
+            for g in range(GROUPS):
+                first_product(0, g, t)
+        weave(nc.vector.tensor_copy, 1, 1, last_pair, 0, 1)
+        weave(nc.vector.tensor_copy, 1, 1, last_pair, 1, 3)
+        weave(nc.scalar.copy, 1, 1, last_pair, 3, GROUPS)
         quantize_picked(1, 0, 1)
+
         late = sbuf("w_bf_late", [P, PACK, P, PACK], BF16)
         for pair in range(2):
             slots = slice(2 * pair, 2 * pair + 2)
-            deal(nc.vector.tensor_copy, late[:, slots, 0:80, :], by_channel(w_last)[:, 0:80, :, slots])
-            deal(nc.scalar.copy, late[:, slots, 80:P, :], by_channel(w_last)[:, 80:P, :, slots])
+            deal(nc.vector.tensor_copy, late[:, slots, 0:80, :], by_channel(w_raw[1])[:, 0:80, :, slots])
+            deal(nc.scalar.copy, late[:, slots, 80:P, :], by_channel(w_raw[1])[:, 80:P, :, slots])
         for t in range(PACK):
-            quantize(slot_codes[1][t], slot_scales[1][t], late[:, t].rearrange("p m j -> p (m j)"))
+            quantize_slot(1, late, t)
         late_codes = sbuf("x_codes_held", [P, 3 * P], U32, "w_bf_late")
         quantize_picked(1, 1, 1, late_codes[:, 0:P])
         quantize_picked(1, 2, 2, late_codes[:, P : 3 * P])
@@ -163,7 +165,8 @@ def tile_picked_haar_gelu_e_kernel(tc, xT, w1, w2_words, w2_scales, w3_words, w3
             codes = [sbuf("band_codes_%d_%d" % (half, b), [P, P], U32) for b in range(2)]
             scales = [sbuf("band_scales_%d_%d" % (half, b), [P, P], U8) for b in range(2)]
             for g in range(2 * half, 2 * half + 2):
-                first_product(1, g)
+                for t in range(PACK):
+                    first_product(1, g, t)
                 stretches = ((0, PAIRS // 2), (PAIRS // 2, PAIRS)) if g < 3 else ((0, PAIRS),)
                 for first, last in stretches:
                     h = sbuf("h_%d_%d" % (g, first), [P, 2, (last - first) * PACK], F32)

@@ -50,18 +50,20 @@ def tile_picked_haar_gelu_e_kernel(tc, xT, w1, w2_words, w2_scales, w3_words, w3
         w_rows = w1.rearrange("(z p j) c -> z p j c", z=2, j=PACK)
         planes = {}
 
-        def load_planes(z, first, count):
+        def load_planes(z, first, count, queue=nc.sync):
             tile = sbuf("x_%d_%d" % (z, first), [P, count, T], F32)
-            nc.sync.dma_start(out=tile[:], in_=x_rows[z][:, first : first + count, :])
+            queue.dma_start(out=tile[:], in_=x_rows[z][:, first : first + count, :])
             for j in range(count):
                 planes[z, first + j] = tile[:, j, :]
 
-        load_planes(0, 0, 4)
+        load_planes(0, 0, 2, nc.scalar)
+        load_planes(0, 2, 2)
         nc.sync.dma_start(offsets[:], offs)
-        load_planes(1, 0, 2)
+        load_planes(1, 0, 1, nc.scalar)
+        load_planes(1, 1, 1)
+        load_planes(1, 2, 1, nc.scalar)
         w_raw = [sbuf("w_raw_%d" % z, [P, PACK, H], F32) for z in range(2)]
         nc.sync.dma_start(out=w_raw[0][:], in_=w_rows[0])
-        load_planes(1, 2, 1)
         load_planes(1, 3, 1)
         nc.sync.dma_start(out=w_raw[1][:], in_=w_rows[1])
         for b, scales in enumerate((w2_scales, w3_scales)):
@@ -129,17 +131,18 @@ def tile_picked_haar_gelu_e_kernel(tc, xT, w1, w2_words, w2_scales, w3_words, w3
         quantize_picked(0, 0, GROUPS)
         weave(nc.vector.tensor_copy, 1, 0, gather_pair(1, 0), 0, GROUPS)
 
-        w_bf = sbuf("w_bf", [P, PACK, P, PACK], BF16)
-        deal(nc.vector.tensor_copy, w_bf[:, :, 0:80, :], by_channel(w_raw[0])[:, 0:80])
-        deal(nc.scalar.copy, w_bf[:, :, 80:P, :], by_channel(w_raw[0])[:, 80:P])
-        for t in range(1, PACK):
+        w_bf = sbuf("w_bf", [P, PACK, P, PACK], BF16, "pair_1_0")
+        for pair in range(2):
+            slots = slice(2 * pair, 2 * pair + 2)
+            deal(nc.vector.tensor_copy, w_bf[:, slots], by_channel(w_raw[0])[:, :, :, slots])
+        for t in (0, 1, 3):
             quantize_slot(0, w_bf, t)
 
         last_pair = sbuf("pair_1_1", [P, 2, S], F32)
         nc.scalar.activation(last_pair[:, 0, :], planes[1, 2].indirect(offsets[:]), COPY)
         nc.vector.tensor_copy(out=last_pair[:, 1, 0:V], in_=planes[1, 3].indirect(offsets[:, 0 : V // 16]))
         nc.scalar.activation(last_pair[:, 1, V:S], planes[1, 3].indirect(offsets[:, V // 16 : S // 16]), COPY)
-        quantize_slot(0, w_bf, 0, "x_1_3")
+        quantize_slot(0, w_bf, 2, "x_1_3")
         for t in range(PACK):
             for g in range(GROUPS):
                 first_product(0, g, t)

@@ -101,7 +101,7 @@ def tile_picked_haar_gelu_e_kernel(tc, xT, w1, w2_words, w2_scales, w3_words, w3
                 x_codes[z, first + g] = codes[:, g * P : (g + 1) * P]
                 x_scales[z, first + g] = scales[:, g * P : (g + 1) * P]
 
-        hidden = [ps.tile([P, PACK, P], F32, name="hidden_%d" % g) for g in range(GROUPS)]
+        hidden = [ps.tile([P, PACK, P], F32, name="hidden_%d" % g) for g in range(GROUPS - 1)]
 
         def first_product(z, g, t):
             nc.tensor.matmul_mx(
@@ -135,16 +135,16 @@ def tile_picked_haar_gelu_e_kernel(tc, xT, w1, w2_words, w2_scales, w3_words, w3
         for pair in range(2):
             slots = slice(2 * pair, 2 * pair + 2)
             deal(nc.vector.tensor_copy, w_bf[:, slots], by_channel(w_raw[0])[:, :, :, slots])
-        for t in (0, 1, 3):
+        for t in (1, 2, 3):
             quantize_slot(0, w_bf, t)
 
         last_pair = sbuf("pair_1_1", [P, 2, S], F32)
         nc.scalar.activation(last_pair[:, 0, :], planes[1, 2].indirect(offsets[:]), COPY)
         nc.vector.tensor_copy(out=last_pair[:, 1, 0:V], in_=planes[1, 3].indirect(offsets[:, 0 : V // 16]))
         nc.scalar.activation(last_pair[:, 1, V:S], planes[1, 3].indirect(offsets[:, V // 16 : S // 16]), COPY)
-        quantize_slot(0, w_bf, 2, "x_1_3")
-        for t in range(PACK):
-            for g in range(GROUPS):
+        quantize_slot(0, w_bf, 0, "x_1_3")
+        for g in range(GROUPS - 1):
+            for t in range(PACK):
                 first_product(0, g, t)
         weave(nc.vector.tensor_copy, 1, 1, last_pair, 0, 1)
         weave(nc.vector.tensor_copy, 1, 1, last_pair, 1, 3)
@@ -168,6 +168,10 @@ def tile_picked_haar_gelu_e_kernel(tc, xT, w1, w2_words, w2_scales, w3_words, w3
             codes = [sbuf("band_codes_%d_%d" % (half, b), [P, P], U32) for b in range(2)]
             scales = [sbuf("band_scales_%d_%d" % (half, b), [P, P], U8) for b in range(2)]
             for g in range(2 * half, 2 * half + 2):
+                if g == GROUPS - 1:
+                    hidden.append(ps.tile([P, PACK, P], F32, name="hidden_last", tag="hidden_0"))
+                    for t in range(PACK):
+                        first_product(0, g, t)
                 for t in range(PACK):
                     first_product(1, g, t)
                 stretches = ((0, PAIRS // 2), (PAIRS // 2, PAIRS)) if g < 3 else ((0, PAIRS),)
@@ -198,11 +202,11 @@ def tile_picked_haar_gelu_e_kernel(tc, xT, w1, w2_words, w2_scales, w3_words, w3
             if half == 0:
                 result = sbuf("result_0", [P, 2, P], F32)
                 for a in range(2):
-                    nc.scalar.mul(result[:, a, :], acc[a][:], 0.5)
+                    nc.scalar.activation(result[:, a, :], acc[a][:], COPY, scale=0.5)
                 nc.sync.dma_start(out=out_rows[:, :, cols], in_=result[:])
             else:
                 results = [sbuf("result_1_%d" % a, [P, P], F32) for a in range(2)]
-                nc.scalar.mul(results[0][:], acc[0][:], 0.5)
+                nc.scalar.activation(results[0][:], acc[0][:], COPY, scale=0.5)
                 nc.scalar.dma_start(out=out_rows[:, 0, cols], in_=results[0][:])
                 nc.vector.tensor_scalar_mul(results[1][:], acc[1][:], 0.5)
                 nc.sync.dma_start(out=out_rows[:, 1, cols], in_=results[1][:])

@@ -147,15 +147,16 @@ def tile_picked_haar_gelu_e_kernel(tc, xT, w1, w2_words, w2_scales, w3_words, w3
             for t in range(PACK):
                 first_product(0, g, t)
         weave(nc.vector.tensor_copy, 1, 1, last_pair, 0, 1)
-        weave(nc.vector.tensor_copy, 1, 1, last_pair, 1, 3)
-        weave(nc.scalar.copy, 1, 1, last_pair, 3, GROUPS)
+        weave(nc.vector.tensor_copy, 1, 1, last_pair, 1, 2)
+        weave(nc.scalar.copy, 1, 1, last_pair, 2, GROUPS)
         quantize_picked(1, 0, 1)
 
         late = sbuf("w_bf_late", [P, PACK, P, PACK], BF16)
         for pair in range(2):
             slots = slice(2 * pair, 2 * pair + 2)
-            deal(nc.vector.tensor_copy, late[:, slots, 0:80, :], by_channel(w_raw[1])[:, 0:80, :, slots])
-            deal(nc.scalar.copy, late[:, slots, 80:P, :], by_channel(w_raw[1])[:, 80:P, :, slots])
+            share = (80, 88)[pair]
+            deal(nc.vector.tensor_copy, late[:, slots, 0:share, :], by_channel(w_raw[1])[:, 0:share, :, slots])
+            deal(nc.scalar.copy, late[:, slots, share:P, :], by_channel(w_raw[1])[:, share:P, :, slots])
         for t in range(PACK):
             quantize_slot(1, late, t)
         late_codes = sbuf("x_codes_held", [P, 3 * P], U32, "w_bf_late")
@@ -164,9 +165,12 @@ def tile_picked_haar_gelu_e_kernel(tc, xT, w1, w2_words, w2_scales, w3_words, w3
 
         out_rows = out.rearrange("(a p) v -> p a v", p=P)
         for half in range(2):
-            bands = [sbuf("band_%d_%d" % (half, b), [P, 2, PAIRS * PACK], BF16) for b in range(2)]
-            codes = [sbuf("band_codes_%d_%d" % (half, b), [P, P], U32) for b in range(2)]
-            scales = [sbuf("band_scales_%d_%d" % (half, b), [P, P], U8) for b in range(2)]
+            both = sbuf("bands_%d" % half, [P, 4 * PAIRS * PACK], BF16)
+            both_codes = sbuf("band_codes_%d" % half, [P, 2 * P], U32)
+            both_scales = sbuf("band_scales_%d" % half, [P, 2 * P], U8)
+            bands = [both[:, b * 512 : (b + 1) * 512].rearrange("p (g e) -> p g e", g=2) for b in range(2)]
+            codes = [both_codes[:, b * P : (b + 1) * P] for b in range(2)]
+            scales = [both_scales[:, b * P : (b + 1) * P] for b in range(2)]
             for g in range(2 * half, 2 * half + 2):
                 if g == GROUPS - 1:
                     hidden.append(ps.tile([P, PACK, P], F32, name="hidden_last", tag="hidden_0"))
@@ -186,15 +190,21 @@ def tile_picked_haar_gelu_e_kernel(tc, xT, w1, w2_words, w2_scales, w3_words, w3
                     for b, op in enumerate((ADD, SUB)):
                         nc.vector.tensor_tensor(bands[b][:, g % 2, first * PACK : last * PACK], h[:, 0, :], h[:, 1, :], op)
             acc = [ps.tile([P, P], F32, name="acc_%d_%d" % (half, a), tag="acc_%d" % a) for a in range(2)]
+            if half == 0:
+                quantize(both_codes[:], both_scales[:], both[:])
             for b in range(2):
-                quantize(codes[b][:], scales[b][:], bands[b][:].rearrange("p g e -> p (g e)"))
+                if half == 1 and b == 1:
+                    for i in range(2):
+                        quantize(codes[b][:, i * PAIRS : (i + 1) * PAIRS], scales[b][:, i * PAIRS : (i + 1) * PAIRS], bands[b][:, i, :])
+                elif half == 1:
+                    quantize(codes[b], scales[b], both[:, 0:512])
                 for a in range(2):
                     nc.tensor.matmul_mx(
                         out=acc[a][:],
                         lhsT=band_words[b][:, a * P : (a + 1) * P].bitcast(FP8X4),
                         lhsT_scale=band_plane[:, b, a * P : (a + 1) * P],
-                        rhs=codes[b][:].bitcast(FP8X4),
-                        rhs_scale=scales[b][:],
+                        rhs=codes[b].bitcast(FP8X4),
+                        rhs_scale=scales[b],
                         start=(b == 0),
                         stop=(b == 1),
                     )

@@ -120,10 +120,10 @@ def tile_picked_haar_gelu_e_kernel(tc, xT, w1, w2_words, w2_scales, w3_words, w3
         def by_channel(raw):
             return raw[:].rearrange("p j (m t) -> p m j t", t=PACK)
 
-        def quantize_slot(z, dealt, t, tag=None):
+        def quantize_slot(z, dealt, t, tag=None, place=None):
             codes = sbuf("w_codes_%d_%d" % (z, t), [P, P], U32, tag)
             scales = sbuf("w_scales_%d_%d" % (z, t), [P, P], U8)
-            quantize(codes[:], scales[:], dealt[:, t].rearrange("p m j -> p (m j)"))
+            quantize(codes[:], scales[:], dealt[:, t if place is None else place].rearrange("p m j -> p (m j)"))
             slot_codes[z, t], slot_scales[z, t] = codes[:], scales[:]
 
         for u in range(2):
@@ -135,33 +135,32 @@ def tile_picked_haar_gelu_e_kernel(tc, xT, w1, w2_words, w2_scales, w3_words, w3
         for pair in range(2):
             slots = slice(2 * pair, 2 * pair + 2)
             deal(nc.vector.tensor_copy, w_bf[:, slots], by_channel(w_raw[0])[:, :, :, slots])
-        for t in (1, 2, 3):
+        for t in (2, 3, 0):
             quantize_slot(0, w_bf, t)
 
         last_pair = sbuf("pair_1_1", [P, 2, S], F32)
         nc.scalar.activation(last_pair[:, 0, :], planes[1, 2].indirect(offsets[:]), COPY)
         nc.vector.tensor_copy(out=last_pair[:, 1, 0:V], in_=planes[1, 3].indirect(offsets[:, 0 : V // 16]))
         nc.scalar.activation(last_pair[:, 1, V:S], planes[1, 3].indirect(offsets[:, V // 16 : S // 16]), COPY)
-        quantize_slot(0, w_bf, 0, "x_1_3")
-        for g in range(GROUPS - 1):
-            for t in range(PACK):
+        quantize_slot(0, w_bf, 1, "x_1_3")
+        for t in range(PACK):
+            for g in range(GROUPS - 1):
                 first_product(0, g, t)
         weave(nc.vector.tensor_copy, 1, 1, last_pair, 0, 1)
         weave(nc.vector.tensor_copy, 1, 1, last_pair, 1, 2)
         weave(nc.scalar.copy, 1, 1, last_pair, 2, GROUPS)
         quantize_picked(1, 0, 1)
 
-        late = sbuf("w_bf_late", [P, PACK, P, PACK], BF16)
+        late = [sbuf("w_bf_late_%d" % pair, [P, 2, P, PACK], BF16) for pair in range(2)]
         for pair in range(2):
             slots = slice(2 * pair, 2 * pair + 2)
             share = (80, 88)[pair]
-            deal(nc.vector.tensor_copy, late[:, slots, 0:share, :], by_channel(w_raw[1])[:, 0:share, :, slots])
-            deal(nc.scalar.copy, late[:, slots, share:P, :], by_channel(w_raw[1])[:, share:P, :, slots])
+            deal(nc.vector.tensor_copy, late[pair][:, :, 0:share, :], by_channel(w_raw[1])[:, 0:share, :, slots])
+            deal(nc.scalar.copy, late[pair][:, :, share:P, :], by_channel(w_raw[1])[:, share:P, :, slots])
         for t in range(PACK):
-            quantize_slot(1, late, t)
-        late_codes = sbuf("x_codes_held", [P, 3 * P], U32, "w_bf_late")
-        quantize_picked(1, 1, 1, late_codes[:, 0:P])
-        quantize_picked(1, 2, 2, late_codes[:, P : 3 * P])
+            quantize_slot(1, late[t // 2], t, None, t % 2)
+        quantize_picked(1, 1, 1, sbuf("x_codes_held_1", [P, P], U32, "w_bf_late_0")[:])
+        quantize_picked(1, 2, 2, sbuf("x_codes_held_2", [P, 2 * P], U32, "w_bf_late_1")[:])
 
         out_rows = out.rearrange("(a p) v -> p a v", p=P)
         for half in range(2):

from contextlib import ExitStack

import concourse.mybir as mybir

K, T, S, V, H, N = 1024, 2048, 512, 256, 512, 256
FLOPS = 2 * K * H * S + 2 * 2 * H * N * V

F32 = mybir.dt.float32
BF16 = mybir.dt.bfloat16
I32 = mybir.dt.int32
U32 = mybir.dt.uint32
U16 = mybir.dt.uint16
U8 = mybir.dt.uint8
FP8X4 = mybir.dt.float8_e4m3fn_x4
GELU = mybir.ActivationFunctionType.Gelu_apprx_tanh
COPY = mybir.ActivationFunctionType.Copy
ADD = mybir.AluOpType.add
SUB = mybir.AluOpType.subtract

P = 128
PACK = 4
K_PASS = P * PACK
GROUPS = 4
PAIRS = V // GROUPS


def tile_picked_haar_gelu_e_kernel(tc, xT, w1, w2_words, w2_scales, w3_words, w3_scales, offs, out):
    nc = tc.nc
    with ExitStack() as ctx:
        sb = ctx.enter_context(tc.tile_pool(name="sb", bufs=1))
        ps = ctx.enter_context(tc.psum_pool(name="ps", bufs=1))

        def sbuf(name, shape, dtype, tag=None):
            return sb.tile(shape, dtype, name=name, tag=tag or name, align_bytes=64)

        def quantize(codes, scales, values):
            nc.vector.quantize_mx(out=codes.bitcast(FP8X4), scales=scales, in_=values)

        offsets = sb.tile([P, S // 16], U16, name="offsets")

        warm_in = sbuf("warm_in", [P, 1], F32)
        warm_out = sbuf("warm_out", [P, 1], F32)
        nc.vector.memset(warm_in[:], 0.0)
        nc.scalar.activation(warm_out[:], warm_in[:], GELU)

        band_plane = sbuf("band_plane", [P, 2, N], U8)
        nc.vector.memset(band_plane[:].rearrange("p b n -> p (b n)").bitcast(I32), 0)

        x_rows = xT.rearrange("(z p j) t -> z p j t", z=2, j=PACK)
        w_rows = w1.rearrange("(z p j) c -> z p j c", z=2, j=PACK)
        planes = {}

        def load_planes(z, first, count, queue=nc.sync):
            tile = sbuf("x_%d_%d" % (z, first), [P, count, T], F32)
            queue.dma_start(out=tile[:], in_=x_rows[z][:, first : first + count, :])
            for j in range(count):
                planes[z, first + j] = tile[:, j, :]

        load_planes(0, 0, 2, nc.scalar)
        load_planes(0, 2, 2)
        nc.sync.dma_start(offsets[:], offs)
        load_planes(1, 0, 1, nc.scalar)
        load_planes(1, 1, 1)
        load_planes(1, 2, 1, nc.scalar)
        w_raw = [sbuf("w_raw_%d" % z, [P, PACK, H], F32) for z in range(2)]
        nc.sync.dma_start(out=w_raw[0][:], in_=w_rows[0])
        load_planes(1, 3, 1)
        nc.sync.dma_start(out=w_raw[1][:], in_=w_rows[1])
        for b, scales in enumerate((w2_scales, w3_scales)):
            for q in range(4):
                nc.sync.dma_start(
                    out=band_plane[32 * q : 32 * q + 4, b, :].bitcast(I32), in_=scales[0, 4 * q : 4 * q + 4, :].bitcast(I32)
                )
        band_words = []
        for name, words in (("w2", w2_words), ("w3", w3_words)):
            tile = sbuf(name + "_codes", [P, N], I32)
            nc.sync.dma_start(out=tile[:], in_=words[0].rearrange("p n r -> p (n r)").bitcast(I32))
            band_words.append(tile)

        slot_codes, slot_scales, x_codes, x_scales = {}, {}, {}, {}
        picked = [sbuf("picked_%d" % z, [P, S, PACK], BF16) for z in range(2)]

        def gather_pair(z, u):
            pair = sbuf("pair_%d_%d" % (z, u), [P, 2, S], F32)
            nc.scalar.activation(pair[:, 0, :], planes[z, 2 * u].indirect(offsets[:]), COPY)
            nc.vector.tensor_copy(out=pair[:, 1, :], in_=planes[z, 2 * u + 1].indirect(offsets[:]))
            return pair

        def weave(engine_copy, z, u, pair, first, last):
            engine_copy(
                out=picked[z][:, :, 2 * u : 2 * u + 2].rearrange("p (g d v) e -> p g d v e", g=GROUPS, d=2)[:, first:last],
                in_=pair[:].rearrange("p e (d g v) -> p g d v e", g=GROUPS, d=2)[:, first:last],
            )

        def quantize_picked(z, first, count, codes=None):
            if codes is None:
                codes = sbuf("x_codes_%d_%d" % (z, first), [P, count * P], U32)[:]
            scales = sbuf("x_scales_%d_%d" % (z, first), [P, count * P], U8)
            quantize(codes, scales[:], picked[z][:, first * P : (first + count) * P, :].rearrange("p s j -> p (s j)"))
            for g in range(count):
                x_codes[z, first + g] = codes[:, g * P : (g + 1) * P]
                x_scales[z, first + g] = scales[:, g * P : (g + 1) * P]

        hidden = [ps.tile([P, PACK, P], F32, name="hidden_%d" % g) for g in range(GROUPS - 1)]

        def first_product(z, g, t):
            nc.tensor.matmul_mx(
                out=hidden[g][:, t, :],
                lhsT=slot_codes[z, t].bitcast(FP8X4),
                lhsT_scale=slot_scales[z, t],
                rhs=x_codes[z, g].bitcast(FP8X4),
                rhs_scale=x_scales[z, g],
                start=(z == 0 and t == 0),
                stop=(z == 1 and t == PACK - 1),
            )

        def deal(engine_copy, target, source):
            engine_copy(out=target.rearrange("p t m j -> p m j t"), in_=source)

        def by_channel(raw):
            return raw[:].rearrange("p j (m t) -> p m j t", t=PACK)

        def quantize_slot(z, dealt, t, tag=None, place=None):
            codes = sbuf("w_codes_%d_%d" % (z, t), [P, P], U32, tag)
            scales = sbuf("w_scales_%d_%d" % (z, t), [P, P], U8)
            quantize(codes[:], scales[:], dealt[:, t if place is None else place].rearrange("p m j -> p (m j)"))
            slot_codes[z, t], slot_scales[z, t] = codes[:], scales[:]

        for u in range(2):
            weave(nc.vector.tensor_copy, 0, u, gather_pair(0, u), 0, GROUPS)
        quantize_picked(0, 0, GROUPS)
        weave(nc.vector.tensor_copy, 1, 0, gather_pair(1, 0), 0, GROUPS)

        w_bf = sbuf("w_bf", [P, PACK, P, PACK], BF16, "pair_1_0")
        for pair in range(2):
            slots = slice(2 * pair, 2 * pair + 2)
            deal(nc.vector.tensor_copy, w_bf[:, slots], by_channel(w_raw[0])[:, :, :, slots])
        for t in (2, 3, 0):
            quantize_slot(0, w_bf, t)

        last_pair = sbuf("pair_1_1", [P, 2, S], F32)
        nc.scalar.activation(last_pair[:, 0, :], planes[1, 2].indirect(offsets[:]), COPY)
        nc.vector.tensor_copy(out=last_pair[:, 1, 0:V], in_=planes[1, 3].indirect(offsets[:, 0 : V // 16]))
        nc.scalar.activation(last_pair[:, 1, V:S], planes[1, 3].indirect(offsets[:, V // 16 : S // 16]), COPY)
        quantize_slot(0, w_bf, 1, "x_1_3")
        for t in range(PACK):
            for g in range(GROUPS - 1):
                first_product(0, g, t)
        weave(nc.vector.tensor_copy, 1, 1, last_pair, 0, 1)
        weave(nc.vector.tensor_copy, 1, 1, last_pair, 1, 2)
        weave(nc.scalar.copy, 1, 1, last_pair, 2, GROUPS)
        quantize_picked(1, 0, 1)

        late = [sbuf("w_bf_late_%d" % pair, [P, 2, P, PACK], BF16) for pair in range(2)]
        for pair in range(2):
            slots = slice(2 * pair, 2 * pair + 2)
            share = (80, 88)[pair]
            deal(nc.vector.tensor_copy, late[pair][:, :, 0:share, :], by_channel(w_raw[1])[:, 0:share, :, slots])
            deal(nc.scalar.copy, late[pair][:, :, share:P, :], by_channel(w_raw[1])[:, share:P, :, slots])
        for t in range(PACK):
            quantize_slot(1, late[t // 2], t, None, t % 2)
        quantize_picked(1, 1, 1, sbuf("x_codes_held_1", [P, P], U32, "w_bf_late_0")[:])
        quantize_picked(1, 2, 2, sbuf("x_codes_held_2", [P, 2 * P], U32, "w_bf_late_1")[:])

        out_rows = out.rearrange("(a p) v -> p a v", p=P)
        for half in range(2):
            both = sbuf("bands_%d" % half, [P, 4 * PAIRS * PACK], BF16)
            both_codes = sbuf("band_codes_%d" % half, [P, 2 * P], U32)
            both_scales = sbuf("band_scales_%d" % half, [P, 2 * P], U8)
            bands = [both[:, b * 512 : (b + 1) * 512].rearrange("p (g e) -> p g e", g=2) for b in range(2)]
            codes = [both_codes[:, b * P : (b + 1) * P] for b in range(2)]
            scales = [both_scales[:, b * P : (b + 1) * P] for b in range(2)]
            for g in range(2 * half, 2 * half + 2):
                if g == GROUPS - 1:
                    hidden.append(ps.tile([P, PACK, P], F32, name="hidden_last", tag="hidden_0"))
                    for t in range(PACK):
                        first_product(0, g, t)
                for t in range(PACK):
                    first_product(1, g, t)
                stretches = ((0, PAIRS // 2), (PAIRS // 2, PAIRS)) if g < 3 else ((0, PAIRS),)
                for first, last in stretches:
                    h = sbuf("h_%d_%d" % (g, first), [P, 2, (last - first) * PACK], F32)
                    nc.scalar.activation(
                        h[:].rearrange("p d (v t) -> p d v t", t=PACK),
                        hidden[g][:].rearrange("p t (d v) -> p d v t", d=2)[:, :, first:last, :],
                        GELU,
                        bias=warm_out[:],
                    )
                    for b, op in enumerate((ADD, SUB)):
                        nc.vector.tensor_tensor(bands[b][:, g % 2, first * PACK : last * PACK], h[:, 0, :], h[:, 1, :], op)
            acc = [ps.tile([P, P], F32, name="acc_%d_%d" % (half, a), tag="acc_%d" % a) for a in range(2)]
            if half == 0:
                quantize(both_codes[:], both_scales[:], both[:])
            for b in range(2):
                if half == 1 and b == 1:
                    for i in range(2):
                        quantize(codes[b][:, i * PAIRS : (i + 1) * PAIRS], scales[b][:, i * PAIRS : (i + 1) * PAIRS], bands[b][:, i, :])
                elif half == 1:
                    quantize(codes[b], scales[b], both[:, 0:512])
                for a in range(2):
                    nc.tensor.matmul_mx(
                        out=acc[a][:],
                        lhsT=band_words[b][:, a * P : (a + 1) * P].bitcast(FP8X4),
                        lhsT_scale=band_plane[:, b, a * P : (a + 1) * P],
                        rhs=codes[b].bitcast(FP8X4),
                        rhs_scale=scales[b],
                        start=(b == 0),
                        stop=(b == 1),
                    )
            cols = slice(half * P, (half + 1) * P)
            if half == 0:
                result = sbuf("result_0", [P, 2, P], F32)
                for a in range(2):
                    nc.scalar.activation(result[:, a, :], acc[a][:], COPY, scale=0.5)
                nc.sync.dma_start(out=out_rows[:, :, cols], in_=result[:])
            else:
                results = [sbuf("result_1_%d" % a, [P, P], F32) for a in range(2)]
                nc.scalar.activation(results[0][:], acc[0][:], COPY, scale=0.5)
                nc.scalar.dma_start(out=out_rows[:, 0, cols], in_=results[0][:])
                nc.vector.tensor_scalar_mul(results[1][:], acc[1][:], 0.5)
                nc.sync.dma_start(out=out_rows[:, 1, cols], in_=results[1][:])
